import numpy as np
import ml_dtypes


def mxq(x, axis, fmt="e4m3"):
    dtype, down = {"e4m3": (ml_dtypes.float8_e4m3fn, 7), "e5m2": (ml_dtypes.float8_e5m2, 14)}[fmt]
    v = np.moveaxis(np.asarray(x, np.float32).astype(ml_dtypes.bfloat16).astype(np.float64), axis, -1)
    blocks = v.reshape(v.shape[:-1] + (-1, 32))
    amax = np.abs(blocks).max(-1, keepdims=True)
    byte = np.maximum(np.where(amax > 0, np.frexp(amax)[1] - 1 + 127, 0) - down, 1)
    scale = np.exp2(byte - 127.0)
    codes = (blocks / scale).astype(np.float32).astype(dtype).astype(np.float64)
    return np.moveaxis((codes * scale).reshape(v.shape), -1, axis)


WIDE = False


def mx_kscale(k):
    if not WIDE:
        return np.ones(k)
    levels = np.array([10, -10, 5, -5, 0])
    if k % 512:
        return np.exp2(np.random.permutation(np.resize(levels, k // 32))).repeat(32)
    a = np.empty((k // 512, 16))
    for p in range(k // 512):
        a[p, :8] = np.random.permutation(np.resize(levels, 8))
        for g in range(8):
            far = levels[np.abs(levels - a[p, g]) >= 10]
            a[p, g + 8] = far[np.random.randint(len(far))]
    return np.exp2(a.ravel()).repeat(32)


def f64(x):
    return np.asarray(x).astype(np.float64)


def striped(idx):
    return np.tile(idx.reshape(-1, 16).T, (8, 1)).astype(np.uint16)


def unstriped(offs):
    return offs[:16].T.reshape(-1).astype(np.int64)


def striped8(idx):
    return np.concatenate([x.reshape(-1, 16).T for x in idx]).astype(np.uint16)


def runs(offs, k):
    lists = np.stack([offs[16 * r : 16 * r + 16].T.reshape(-1) for r in range(8)]).astype(np.int64)
    return lists[np.arange(k) % 512 // 64]


def pack_weight(w):
    k, n = w.shape
    w = f64(np.asarray(w, np.float32).astype(ml_dtypes.bfloat16)).reshape(k // 32, 32, n)
    amax = np.abs(w).max(1)
    byte = np.clip(np.where(amax > 0, np.frexp(amax)[1] - 1 + 127 - 7, 1), 1, 254)
    scaled = (w * np.exp2(127.0 - byte)[:, None, :]).reshape(k, n).astype(np.float32)
    words = np.ascontiguousarray(scaled.reshape(k // 512, 128, 4, n).transpose(0, 1, 3, 2)).astype(ml_dtypes.float8_e4m3fn).view(np.uint8)
    return words, np.ascontiguousarray(byte.astype(np.uint8).reshape(k // 512, 16, n))


def unpack_weight(words, scales):
    g, p, n, _ = words.shape
    vals = np.ascontiguousarray(words).view(ml_dtypes.float8_e4m3fn).astype(np.float64) * np.repeat(np.exp2(scales.astype(np.float64) - 127.0), 8, axis=1)[..., None]
    return vals.transpose(0, 1, 3, 2).reshape(g * 512, n)

def planes(y):
    n, m = y.shape
    v = y.astype(np.float32).astype(ml_dtypes.bfloat16).astype(np.float64).reshape(n // 32, 32, m)
    top = np.abs(v).max(1)
    byte = np.clip(np.where(top > 0, np.frexp(top)[1] - 1 + 127 - 7, 1), 1, 254)
    codes = (v * np.exp2(127.0 - byte)[:, None, :]).reshape(n, m).astype(np.float32).astype(ml_dtypes.float8_e4m3fn).view(np.uint8)
    words = codes.reshape(n // 512, 128, 4, m).transpose(0, 1, 3, 2)
    return np.ascontiguousarray(words), np.ascontiguousarray(byte.astype(np.uint8).reshape(n // 512, 16, m))


K, T, S, V, G, H = 512, 2048, 512, 256, 2048, 512


def setup_inputs():
    n = np.random.standard_normal
    s = mx_kscale(K)[:, None]
    packed_xT = pack_weight(n((K, T)) * s)
    packed_dT = pack_weight(n((K, G)) / s)
    perm = np.stack([np.random.permutation(S) for _ in range(8)])
    return {
        "x_words": packed_xT[0],
        "x_scales": packed_xT[1],
        "d_words": packed_dT[0],
        "d_scales": packed_dT[1],
        "gs": (np.random.uniform(0.5, 1.5, (K, 1)) * s).astype(np.float32),
        "offs": striped(np.random.permutation(T)[:S]),
        "k1": striped8(np.random.randint(0, G, (8, H))),
        "la": striped8(perm[:, :V]),
        "lb": striped8(perm[:, V:]),
        "k2": striped8(np.random.randint(0, G, (8, H))),
    }


def reference(x_words, x_scales, d_words, d_scales, gs, offs, k1, la, lb, k2):
    d_k2 = unpack_weight(d_words, d_scales)[np.arange(K)[:, None], runs(k2, K)]
    d_k1 = unpack_weight(d_words, d_scales)[np.arange(K)[:, None], runs(k1, K)]
    xq = unpack_weight(x_words, x_scales)[:, unstriped(offs)]
    h = 0.0625 * (d_k1.T @ xq)
    p = h[np.arange(H)[:, None], runs(la, H)]
    qv = h[np.arange(H)[:, None], runs(lb, H)]
    lo = np.minimum(p, qv)
    hi = np.maximum(p, qv)
    d1 = np.zeros((H, S))
    d1[np.arange(H)[:, None], runs(la, H)] = hi
    d2 = d1.copy()
    d2[np.arange(H)[:, None], runs(lb, H)] = lo
    z = f64(gs) * d2
    out_0 = 0.0625 * ((d_k2.T @ mxq(z, 0, "e4m3")))
    return (out_0,) + planes(out_0)

@@ -1,0 +1,175 @@
+from contextlib import ExitStack
+
+import concourse.mybir as mybir
+
+F32 = mybir.dt.float32
+BF16 = mybir.dt.bfloat16
+I32 = mybir.dt.int32
+U32 = mybir.dt.uint32
+U16 = mybir.dt.uint16
+U8 = mybir.dt.uint8
+FP8X4 = mybir.dt.float8_e4m3fn_x4
+ALU = mybir.AluOpType
+COPY = mybir.ActivationFunctionType.Copy
+
+P = 128
+PACK = 4
+TABLE = 2048
+S = 512
+V = 256
+CHUNK = 128
+CHUNKS = S // CHUNK
+SIXTEENTH = 0.0625
+
+FLOPS = 2 * 2 * 512 * 512 * 512
+
+
+def tile_picked_pqord_none_po_kernel(
+    tc, x_words, x_scales, d_words, d_scales, gs, offs, k1, la, lb, k2, out_0, out_1, out_2
+):
+    nc = tc.nc
+    with ExitStack() as ctx:
+        lists = ctx.enter_context(tc.tile_pool(name="lists", bufs=1))
+        keep = ctx.enter_context(tc.tile_pool(name="keep", bufs=1))
+        psum = ctx.enter_context(tc.psum_pool(name="psum", bufs=1))
+
+        def sb(name, shape, dtype):
+            return keep.tile(shape, dtype, name=name, align_bytes=64)
+
+        k1_t = lists.tile([P, S // 16], U16, name="k1_t")
+        k2_t = lists.tile([P, S // 16], U16, name="k2_t")
+        offs_t = lists.tile([P, S // 16], U16, name="offs_t")
+        la_t = lists.tile([P, V // 16], U16, name="la_t")
+        lb_t = lists.tile([P, V // 16], U16, name="lb_t")
+
+        d_wtab = sb("d_wtab", [P, TABLE], U32)
+        x_wtab = keep.tile([P, TABLE], U32, name="x_wtab", tag="slot_xw", align_bytes=64)
+        d_stab = keep.tile([P, TABLE], U8, name="d_stab", tag="slot_ds", align_bytes=64)
+        x_stab = keep.tile([P, TABLE], U8, name="x_stab", tag="slot_xs", align_bytes=64)
+        gs_t = sb("gs_t", [P, PACK], F32)
+        gz = sb("gz", [P, PACK], F32)
+        picked_bytes = sb("picked_bytes", [P, 3 * S], U8)
+        placed = sb("placed", [P, 3 * S], U8)
+        dealt_bytes = sb("dealt_bytes", [P, 3 * S], U8)
+
+        nc.vector.memset(placed[:].bitcast(I32), 0)
+
+        def rows_by_block(scales):
+            return scales[0].bitcast(I32).unsqueeze(1).to_broadcast([16, 8, TABLE // 4])
+
+        nc.sync.dma_start(k1_t[:], k1)
+        nc.sync.dma_start(d_stab[:].bitcast(I32), rows_by_block(d_scales))
+        nc.sync.dma_start(k2_t[:], k2)
+        nc.sync.dma_start(x_stab[:].bitcast(I32), rows_by_block(x_scales))
+        nc.sync.dma_start(offs_t[:], offs)
+        nc.sync.dma_start(d_wtab[:].bitcast(I32), d_words[0].rearrange("p n t -> p (n t)").bitcast(I32))
+        nc.sync.dma_start(x_wtab[:].bitcast(I32), x_words[0].rearrange("p n t -> p (n t)").bitcast(I32))
+        nc.sync.dma_start(la_t[:], la)
+        nc.sync.dma_start(lb_t[:], lb)
+        nc.gpsimd.dma_start(gs_t[:], gs.rearrange("(p t) o -> p (t o)", t=PACK))
+        nc.gpsimd.tensor_scalar(gz[:], gs_t[:], SIXTEENTH, 0.0, ALU.mult, ALU.add)
+
+        def deal(dst, src):
+            nc.vector.tensor_copy(dst.rearrange("p (t c i) -> p c t i", t=PACK, i=4), src.rearrange("p (c i t) -> p c t i", t=PACK, i=4))
+
+        def coded_words(i, codes, slot):
+            picked = keep.tile([P, S], U32, name=f"w_words{i}", tag=slot, align_bytes=64)
+            dealt = sb(f"w_words_dealt{i}", [P, S], U32)
+            nc.vector.tensor_copy(picked[:], d_wtab[:].indirect(codes[:]))
+            deal(dealt[:].bitcast(I32), picked[:].bitcast(I32))
+            return dealt
+
+        nc.vector.tensor_copy(picked_bytes[:, 0:S], d_stab[:].indirect(k1_t[:]))
+        nc.vector.tensor_copy(picked_bytes[:, S : 2 * S], d_stab[:].indirect(k2_t[:]))
+        nc.vector.tensor_copy(picked_bytes[:, 2 * S : 3 * S], x_stab[:].indirect(offs_t[:]))
+        nc.vector.tensor_copy(
+            dealt_bytes[:, 0 : 2 * S].rearrange("p (w t c i) -> p w c t i", w=2, t=PACK, i=16),
+            picked_bytes[:, 0 : 2 * S].rearrange("p (w c i t) -> p w c t i", w=2, t=PACK, i=16),
+        )
+        nc.vector.tensor_copy(dealt_bytes[:, 2 * S : 3 * S].bitcast(I32), picked_bytes[:, 2 * S : 3 * S].bitcast(I32))
+        for j in range(4):
+            nc.scalar.dma_start(placed[j:P:32, :].bitcast(I32), dealt_bytes[8 * j : P : 32, :].bitcast(I32))
+        x_plane = placed[:, 2 * S : 3 * S]
+        w1 = coded_words(0, k1_t, "slot_xs")
+        x_codes = keep.tile([P, S], U32, name="x_codes", tag="slot_ds", align_bytes=64)
+        nc.vector.tensor_copy(x_codes[:], x_wtab[:].indirect(offs_t[:]))
+
+        h = [sb(f"h{t}", [P, S], F32) for t in range(PACK)]
+        for t in range(PACK):
+            cols = slice(P * t, P * (t + 1))
+            acc = psum.tile([P, S], F32, name=f"h_acc{t}")
+            nc.tensor.matmul_mx(
+                out=acc[:], lhsT=w1[:, cols].bitcast(FP8X4), lhsT_scale=placed[:, cols],
+                rhs=x_codes[:].bitcast(FP8X4), rhs_scale=x_plane, start=True, stop=True,
+            )
+            nc.scalar.copy(h[t][:], acc[:])
+
+        w2 = coded_words(1, k2_t, "slot_xw")
+
+        d2 = [sb(f"d2_{t}", [P, S], F32) for t in range(PACK)]
+        z = sb("z", [P, S, PACK], BF16)
+        for u in range(2):
+            ts = (2 * u, 2 * u + 1)
+            pa = sb(f"pa{u}", [P, 2, V], F32)
+            pb = sb(f"pb{u}", [P, 2, V], F32)
+            hi = sb(f"hi{u}", [P, 2, V], F32)
+            lo = sb(f"lo{u}", [P, 2, V], F32)
+            for e, t in enumerate(ts):
+                nc.vector.tensor_copy(pa[:, e, :], h[t][:].indirect(la_t[:]))
+                nc.vector.tensor_copy(pb[:, e, :], h[t][:].indirect(lb_t[:]))
+            nc.vector.tensor_tensor(hi[:], pa[:], pb[:], ALU.max)
+            nc.vector.tensor_tensor(lo[:], pa[:], pb[:], ALU.min)
+            for e, t in enumerate(ts):
+                nc.vector.tensor_copy(d2[t][:].indirect(la_t[:]), hi[:, e, :])
+            for e, t in enumerate(ts):
+                nc.vector.tensor_copy(d2[t][:].indirect(lb_t[:]), lo[:, e, :])
+            if u == 0:
+                for t in ts:
+                    nc.scalar.activation(z[:, :, t], d2[t][:], COPY, scale=gz[:, t : t + 1])
+
+        nc.scalar.activation(z[:, :, 2], d2[2][:], COPY, scale=gz[:, 2:3])
+        for c in range(CHUNKS):
+            cols = slice(CHUNK * c, CHUNK * (c + 1))
+            nc.scalar.activation(z[:, cols, 3], d2[3][:, cols], COPY, scale=gz[:, 3:4])
+
+        z_codes = sb("z_codes", [P, S], U32)
+        z_plane = sb("z_plane", [P, S], U8)
+        y_codes = sb("y_codes", [P, S], U32)
+        y_plane = sb("y_plane", [P, S], U8)
+        y = [sb(f"y{c}", [P, PACK, CHUNK], F32) for c in range(CHUNKS)]
+        y_bf = sb("y_bf", [P, S, PACK], BF16)
+        out_rows = out_0.rearrange("(p t) j -> p t j", t=PACK)
+        out_words = out_1[0].rearrange("p n t -> p (n t)").bitcast(I32)
+
+        def second_product(c):
+            cols = slice(CHUNK * c, CHUNK * (c + 1))
+            nc.vector.quantize_mx(
+                out=z_codes[:, cols].bitcast(FP8X4), scales=z_plane[:, cols],
+                in_=z[:, cols, :].rearrange("p n t -> p (n t)"),
+            )
+            acc = psum.tile([P, PACK, CHUNK], F32, name=f"y_acc{c}")
+            for t in range(PACK):
+                rows = slice(P * t, P * (t + 1))
+                nc.tensor.matmul_mx(
+                    out=acc[:, t, :], lhsT=w2[:, rows].bitcast(FP8X4), lhsT_scale=placed[:, S + P * t : S + P * (t + 1)],
+                    rhs=z_codes[:, cols].bitcast(FP8X4), rhs_scale=z_plane[:, cols], start=True, stop=True,
+                )
+            nc.scalar.activation(y[c][:], acc[:], COPY, scale=SIXTEENTH)
+            nc.sync.dma_start(out_rows[:, :, cols], y[c][:])
+
+        for c in range(CHUNKS):
+            second_product(c)
+
+        for c in range(CHUNKS):
+            cols = slice(CHUNK * c, CHUNK * (c + 1))
+            nc.vector.tensor_copy(y_bf[:, cols, :].rearrange("p (c i) t -> p c t i", i=4), y[c][:].rearrange("p t (c i) -> p c t i", i=4))
+            nc.vector.quantize_mx(
+                out=y_codes[:, cols].bitcast(FP8X4), scales=y_plane[:, cols],
+                in_=y_bf[:, cols, :].rearrange("p n t -> p (n t)"),
+            )
+            if c % 2 == 1:
+                cols = slice(CHUNK * (c - 1), CHUNK * (c + 1))
+                nc.sync.dma_start(out_words[:, cols], y_codes[:, cols].bitcast(I32))
+        for q in range(4):
+            eng = nc.scalar if q % 2 == 0 else nc.sync
+            eng.dma_start(out_2[0].bitcast(I32)[4 * q : 4 * q + 4, :], y_plane[32 * q : 32 * q + 4, :].bitcast(I32))

@@ -47,37 +47,27 @@ def tile_picked_pqord_none_po_kernel(
         d_stab = keep.tile([P, TABLE], U8, name="d_stab", tag="slot_ds", align_bytes=64)
         x_stab = keep.tile([P, TABLE], U8, name="x_stab", tag="slot_xs", align_bytes=64)
         gs_t = sb("gs_t", [P, PACK], F32)
-        gz = sb("gz", [P, PACK], F32)
         picked_bytes = sb("picked_bytes", [P, 3 * S], U8)
         placed = sb("placed", [P, 3 * S], U8)
         dealt_bytes = sb("dealt_bytes", [P, 3 * S], U8)
 
+        nc.vector.memset(d_stab[:].bitcast(I32), 0)
+        nc.vector.memset(x_stab[:].bitcast(I32), 0)
         nc.vector.memset(placed[:].bitcast(I32), 0)
 
-        def rows_by_block(scales):
-            return scales[0].bitcast(I32).unsqueeze(1).to_broadcast([16, 8, TABLE // 4])
-
+        nc.scalar.dma_start(d_stab[0:P:8, :].bitcast(I32), d_scales[0].bitcast(I32))
+        nc.scalar.dma_start(x_stab[0:P:8, :].bitcast(I32), x_scales[0].bitcast(I32))
         nc.sync.dma_start(k1_t[:], k1)
-        nc.sync.dma_start(d_stab[:].bitcast(I32), rows_by_block(d_scales))
         nc.sync.dma_start(k2_t[:], k2)
-        nc.sync.dma_start(x_stab[:].bitcast(I32), rows_by_block(x_scales))
         nc.sync.dma_start(offs_t[:], offs)
-        nc.sync.dma_start(d_wtab[:].bitcast(I32), d_words[0].rearrange("p n t -> p (n t)").bitcast(I32))
-        nc.sync.dma_start(x_wtab[:].bitcast(I32), x_words[0].rearrange("p n t -> p (n t)").bitcast(I32))
         nc.sync.dma_start(la_t[:], la)
         nc.sync.dma_start(lb_t[:], lb)
+        nc.sync.dma_start(d_wtab[:].bitcast(I32), d_words[0].rearrange("p n t -> p (n t)").bitcast(I32))
+        nc.sync.dma_start(x_wtab[:].bitcast(I32), x_words[0].rearrange("p n t -> p (n t)").bitcast(I32))
         nc.gpsimd.dma_start(gs_t[:], gs.rearrange("(p t) o -> p (t o)", t=PACK))
-        nc.gpsimd.tensor_scalar(gz[:], gs_t[:], SIXTEENTH, 0.0, ALU.mult, ALU.add)
 
         def deal(dst, src):
             nc.vector.tensor_copy(dst.rearrange("p (t c i) -> p c t i", t=PACK, i=4), src.rearrange("p (c i t) -> p c t i", t=PACK, i=4))
-
-        def coded_words(i, codes, slot):
-            picked = keep.tile([P, S], U32, name=f"w_words{i}", tag=slot, align_bytes=64)
-            dealt = sb(f"w_words_dealt{i}", [P, S], U32)
-            nc.vector.tensor_copy(picked[:], d_wtab[:].indirect(codes[:]))
-            deal(dealt[:].bitcast(I32), picked[:].bitcast(I32))
-            return dealt
 
         nc.vector.tensor_copy(picked_bytes[:, 0:S], d_stab[:].indirect(k1_t[:]))
         nc.vector.tensor_copy(picked_bytes[:, S : 2 * S], d_stab[:].indirect(k2_t[:]))
@@ -90,47 +80,48 @@ def tile_picked_pqord_none_po_kernel(
         for j in range(4):
             nc.scalar.dma_start(placed[j:P:32, :].bitcast(I32), dealt_bytes[8 * j : P : 32, :].bitcast(I32))
         x_plane = placed[:, 2 * S : 3 * S]
-        w1 = coded_words(0, k1_t, "slot_xs")
+        w1_picked = keep.tile([P, S], U32, name="w1_picked", tag="slot_xs", align_bytes=64)
+        w1 = sb("w1", [P, S], U32)
+        nc.vector.tensor_copy(w1_picked[:], d_wtab[:].indirect(k1_t[:]))
+        deal(w1[:].bitcast(I32), w1_picked[:].bitcast(I32))
         x_codes = keep.tile([P, S], U32, name="x_codes", tag="slot_ds", align_bytes=64)
         nc.vector.tensor_copy(x_codes[:], x_wtab[:].indirect(offs_t[:]))
 
-        h = [sb(f"h{t}", [P, S], F32) for t in range(PACK)]
+        h = [keep.tile([P, S], F32, name=f"h{t}", tag=f"slot_h{t}", align_bytes=64) for t in range(PACK)]
         for t in range(PACK):
-            cols = slice(P * t, P * (t + 1))
+            rows = slice(P * t, P * (t + 1))
             acc = psum.tile([P, S], F32, name=f"h_acc{t}")
             nc.tensor.matmul_mx(
-                out=acc[:], lhsT=w1[:, cols].bitcast(FP8X4), lhsT_scale=placed[:, cols],
+                out=acc[:], lhsT=w1[:, rows].bitcast(FP8X4), lhsT_scale=placed[:, rows],
                 rhs=x_codes[:].bitcast(FP8X4), rhs_scale=x_plane, start=True, stop=True,
             )
-            nc.scalar.copy(h[t][:], acc[:])
+            nc.scalar.activation(h[t][:], acc[:], COPY, scale=SIXTEENTH)
 
-        w2 = coded_words(1, k2_t, "slot_xw")
+        w2_picked = keep.tile([P, S], U32, name="w2_picked", tag="slot_xw", align_bytes=64)
+        nc.vector.tensor_copy(w2_picked[:], d_wtab[:].indirect(k2_t[:]))
 
         d2 = [sb(f"d2_{t}", [P, S], F32) for t in range(PACK)]
         z = sb("z", [P, S, PACK], BF16)
-        for u in range(2):
-            ts = (2 * u, 2 * u + 1)
-            pa = sb(f"pa{u}", [P, 2, V], F32)
-            pb = sb(f"pb{u}", [P, 2, V], F32)
-            hi = sb(f"hi{u}", [P, 2, V], F32)
-            lo = sb(f"lo{u}", [P, 2, V], F32)
-            for e, t in enumerate(ts):
-                nc.vector.tensor_copy(pa[:, e, :], h[t][:].indirect(la_t[:]))
-                nc.vector.tensor_copy(pb[:, e, :], h[t][:].indirect(lb_t[:]))
-            nc.vector.tensor_tensor(hi[:], pa[:], pb[:], ALU.max)
-            nc.vector.tensor_tensor(lo[:], pa[:], pb[:], ALU.min)
-            for e, t in enumerate(ts):
-                nc.vector.tensor_copy(d2[t][:].indirect(la_t[:]), hi[:, e, :])
-            for e, t in enumerate(ts):
-                nc.vector.tensor_copy(d2[t][:].indirect(lb_t[:]), lo[:, e, :])
-            if u == 0:
-                for t in ts:
-                    nc.scalar.activation(z[:, :, t], d2[t][:], COPY, scale=gz[:, t : t + 1])
-
-        nc.scalar.activation(z[:, :, 2], d2[2][:], COPY, scale=gz[:, 2:3])
+        pa = sb("pa", [P, PACK, V], F32)
+        pb = sb("pb", [P, PACK, V], F32)
+        hi = sb("hi", [P, PACK, V], F32)
+        lo = sb("lo", [P, PACK, V], F32)
+        for t in range(PACK):
+            nc.vector.tensor_copy(pa[:, t, :], h[t][:].indirect(la_t[:]))
+            nc.vector.tensor_copy(pb[:, t, :], h[t][:].indirect(lb_t[:]))
+        w2 = keep.tile([P, S], U32, name="w2", tag="slot_h2", align_bytes=64)
+        deal(w2[:].bitcast(I32), w2_picked[:].bitcast(I32))
+        nc.vector.tensor_tensor(hi[:], pa[:], pb[:], ALU.max)
+        nc.vector.tensor_tensor(lo[:], pa[:], pb[:], ALU.min)
+        for t in range(PACK):
+            nc.vector.tensor_copy(d2[t][:].indirect(la_t[:]), hi[:, t, :])
+        for t in range(PACK):
+            nc.vector.tensor_copy(d2[t][:].indirect(lb_t[:]), lo[:, t, :])
+        for t in range(PACK - 1):
+            nc.scalar.activation(z[:, :, t], d2[t][:], COPY, scale=gs_t[:, t : t + 1])
         for c in range(CHUNKS):
             cols = slice(CHUNK * c, CHUNK * (c + 1))
-            nc.scalar.activation(z[:, cols, 3], d2[3][:, cols], COPY, scale=gz[:, 3:4])
+            nc.scalar.activation(z[:, cols, 3], d2[3][:, cols], COPY, scale=gs_t[:, 3:4])
 
         z_codes = sb("z_codes", [P, S], U32)
         z_plane = sb("z_plane", [P, S], U8)

from contextlib import ExitStack

import concourse.mybir as mybir

F32 = mybir.dt.float32
BF16 = mybir.dt.bfloat16
I32 = mybir.dt.int32
U32 = mybir.dt.uint32
U16 = mybir.dt.uint16
U8 = mybir.dt.uint8
FP8X4 = mybir.dt.float8_e4m3fn_x4
ALU = mybir.AluOpType
COPY = mybir.ActivationFunctionType.Copy

P = 128
PACK = 4
TABLE = 2048
S = 512
V = 256
CHUNK = 128
CHUNKS = S // CHUNK
SIXTEENTH = 0.0625

FLOPS = 2 * 2 * 512 * 512 * 512


def tile_picked_pqord_none_po_kernel(
    tc, x_words, x_scales, d_words, d_scales, gs, offs, k1, la, lb, k2, out_0, out_1, out_2
):
    nc = tc.nc
    with ExitStack() as ctx:
        lists = ctx.enter_context(tc.tile_pool(name="lists", bufs=1))
        keep = ctx.enter_context(tc.tile_pool(name="keep", bufs=1))
        psum = ctx.enter_context(tc.psum_pool(name="psum", bufs=1))

        def sb(name, shape, dtype):
            return keep.tile(shape, dtype, name=name, align_bytes=64)

        k1_t = lists.tile([P, S // 16], U16, name="k1_t")
        k2_t = lists.tile([P, S // 16], U16, name="k2_t")
        offs_t = lists.tile([P, S // 16], U16, name="offs_t")
        la_t = lists.tile([P, V // 16], U16, name="la_t")
        lb_t = lists.tile([P, V // 16], U16, name="lb_t")

        d_wtab = sb("d_wtab", [P, TABLE], U32)
        x_wtab = keep.tile([P, TABLE], U32, name="x_wtab", tag="slot_xw", align_bytes=64)
        d_stab = keep.tile([P, TABLE], U8, name="d_stab", tag="slot_ds", align_bytes=64)
        x_stab = keep.tile([P, TABLE], U8, name="x_stab", tag="slot_xs", align_bytes=64)
        gs_t = sb("gs_t", [P, PACK], F32)
        picked_bytes = sb("picked_bytes", [P, 3 * S], U8)
        placed = sb("placed", [P, 3 * S], U8)
        dealt_bytes = sb("dealt_bytes", [P, 3 * S], U8)

        nc.vector.memset(d_stab[:].bitcast(I32), 0)
        nc.vector.memset(x_stab[:].bitcast(I32), 0)
        nc.vector.memset(placed[:].bitcast(I32), 0)

        nc.scalar.dma_start(d_stab[0:P:8, :].bitcast(I32), d_scales[0].bitcast(I32))
        nc.scalar.dma_start(x_stab[0:P:8, :].bitcast(I32), x_scales[0].bitcast(I32))
        nc.sync.dma_start(k1_t[:], k1)
        nc.sync.dma_start(k2_t[:], k2)
        nc.sync.dma_start(offs_t[:], offs)
        nc.sync.dma_start(la_t[:], la)
        nc.sync.dma_start(lb_t[:], lb)
        nc.sync.dma_start(d_wtab[:].bitcast(I32), d_words[0].rearrange("p n t -> p (n t)").bitcast(I32))
        nc.sync.dma_start(x_wtab[:].bitcast(I32), x_words[0].rearrange("p n t -> p (n t)").bitcast(I32))
        nc.gpsimd.dma_start(gs_t[:], gs.rearrange("(p t) o -> p (t o)", t=PACK))

        def deal(dst, src):
            nc.vector.tensor_copy(dst.rearrange("p (t c i) -> p c t i", t=PACK, i=4), src.rearrange("p (c i t) -> p c t i", t=PACK, i=4))

        nc.vector.tensor_copy(picked_bytes[:, 0:S], d_stab[:].indirect(k1_t[:]))
        nc.vector.tensor_copy(picked_bytes[:, S : 2 * S], d_stab[:].indirect(k2_t[:]))
        nc.vector.tensor_copy(picked_bytes[:, 2 * S : 3 * S], x_stab[:].indirect(offs_t[:]))
        nc.vector.tensor_copy(
            dealt_bytes[:, 0 : 2 * S].rearrange("p (w t c i) -> p w c t i", w=2, t=PACK, i=16),
            picked_bytes[:, 0 : 2 * S].rearrange("p (w c i t) -> p w c t i", w=2, t=PACK, i=16),
        )
        nc.vector.tensor_copy(dealt_bytes[:, 2 * S : 3 * S].bitcast(I32), picked_bytes[:, 2 * S : 3 * S].bitcast(I32))
        for j in range(4):
            nc.scalar.dma_start(placed[j:P:32, :].bitcast(I32), dealt_bytes[8 * j : P : 32, :].bitcast(I32))
        x_plane = placed[:, 2 * S : 3 * S]
        w1_picked = keep.tile([P, S], U32, name="w1_picked", tag="slot_xs", align_bytes=64)
        w1 = sb("w1", [P, S], U32)
        nc.vector.tensor_copy(w1_picked[:], d_wtab[:].indirect(k1_t[:]))
        deal(w1[:].bitcast(I32), w1_picked[:].bitcast(I32))
        x_codes = keep.tile([P, S], U32, name="x_codes", tag="slot_ds", align_bytes=64)
        nc.vector.tensor_copy(x_codes[:], x_wtab[:].indirect(offs_t[:]))

        h = [keep.tile([P, S], F32, name=f"h{t}", tag=f"slot_h{t}", align_bytes=64) for t in range(PACK)]
        for t in range(PACK):
            rows = slice(P * t, P * (t + 1))
            acc = psum.tile([P, S], F32, name=f"h_acc{t}")
            nc.tensor.matmul_mx(
                out=acc[:], lhsT=w1[:, rows].bitcast(FP8X4), lhsT_scale=placed[:, rows],
                rhs=x_codes[:].bitcast(FP8X4), rhs_scale=x_plane, start=True, stop=True,
            )
            nc.scalar.activation(h[t][:], acc[:], COPY, scale=SIXTEENTH)

        w2_picked = keep.tile([P, S], U32, name="w2_picked", tag="slot_xw", align_bytes=64)
        nc.vector.tensor_copy(w2_picked[:], d_wtab[:].indirect(k2_t[:]))

        d2 = [sb(f"d2_{t}", [P, S], F32) for t in range(PACK)]
        z = sb("z", [P, S, PACK], BF16)
        pa = sb("pa", [P, PACK, V], F32)
        pb = sb("pb", [P, PACK, V], F32)
        hi = sb("hi", [P, PACK, V], F32)
        lo = sb("lo", [P, PACK, V], F32)
        for t in range(PACK):
            nc.vector.tensor_copy(pa[:, t, :], h[t][:].indirect(la_t[:]))
            nc.vector.tensor_copy(pb[:, t, :], h[t][:].indirect(lb_t[:]))
        w2 = keep.tile([P, S], U32, name="w2", tag="slot_h2", align_bytes=64)
        deal(w2[:].bitcast(I32), w2_picked[:].bitcast(I32))
        nc.vector.tensor_tensor(hi[:], pa[:], pb[:], ALU.max)
        nc.vector.tensor_tensor(lo[:], pa[:], pb[:], ALU.min)
        for t in range(PACK):
            nc.vector.tensor_copy(d2[t][:].indirect(la_t[:]), hi[:, t, :])
        for t in range(PACK):
            nc.vector.tensor_copy(d2[t][:].indirect(lb_t[:]), lo[:, t, :])
        for t in range(PACK - 1):
            nc.scalar.activation(z[:, :, t], d2[t][:], COPY, scale=gs_t[:, t : t + 1])
        for c in range(CHUNKS):
            cols = slice(CHUNK * c, CHUNK * (c + 1))
            nc.scalar.activation(z[:, cols, 3], d2[3][:, cols], COPY, scale=gs_t[:, 3:4])

        z_codes = sb("z_codes", [P, S], U32)
        z_plane = sb("z_plane", [P, S], U8)
        y_codes = sb("y_codes", [P, S], U32)
        y_plane = sb("y_plane", [P, S], U8)
        y = [sb(f"y{c}", [P, PACK, CHUNK], F32) for c in range(CHUNKS)]
        y_bf = sb("y_bf", [P, S, PACK], BF16)
        out_rows = out_0.rearrange("(p t) j -> p t j", t=PACK)
        out_words = out_1[0].rearrange("p n t -> p (n t)").bitcast(I32)

        def second_product(c):
            cols = slice(CHUNK * c, CHUNK * (c + 1))
            nc.vector.quantize_mx(
                out=z_codes[:, cols].bitcast(FP8X4), scales=z_plane[:, cols],
                in_=z[:, cols, :].rearrange("p n t -> p (n t)"),
            )
            acc = psum.tile([P, PACK, CHUNK], F32, name=f"y_acc{c}")
            for t in range(PACK):
                rows = slice(P * t, P * (t + 1))
                nc.tensor.matmul_mx(
                    out=acc[:, t, :], lhsT=w2[:, rows].bitcast(FP8X4), lhsT_scale=placed[:, S + P * t : S + P * (t + 1)],
                    rhs=z_codes[:, cols].bitcast(FP8X4), rhs_scale=z_plane[:, cols], start=True, stop=True,
                )
            nc.scalar.activation(y[c][:], acc[:], COPY, scale=SIXTEENTH)
            nc.sync.dma_start(out_rows[:, :, cols], y[c][:])

        for c in range(CHUNKS):
            second_product(c)

        for c in range(CHUNKS):
            cols = slice(CHUNK * c, CHUNK * (c + 1))
            nc.vector.tensor_copy(y_bf[:, cols, :].rearrange("p (c i) t -> p c t i", i=4), y[c][:].rearrange("p t (c i) -> p c t i", i=4))
            nc.vector.quantize_mx(
                out=y_codes[:, cols].bitcast(FP8X4), scales=y_plane[:, cols],
                in_=y_bf[:, cols, :].rearrange("p n t -> p (n t)"),
            )
            if c % 2 == 1:
                cols = slice(CHUNK * (c - 1), CHUNK * (c + 1))
                nc.sync.dma_start(out_words[:, cols], y_codes[:, cols].bitcast(I32))
        for q in range(4):
            eng = nc.scalar if q % 2 == 0 else nc.sync
            eng.dma_start(out_2[0].bitcast(I32)[4 * q : 4 * q + 4, :], y_plane[32 * q : 32 * q + 4, :].bitcast(I32))
